import numpy as np
import ml_dtypes


def mxq(x, axis, fmt="e4m3"):
    dtype, down = {"e4m3": (ml_dtypes.float8_e4m3fn, 7), "e5m2": (ml_dtypes.float8_e5m2, 14)}[fmt]
    v = np.moveaxis(np.asarray(x, np.float32).astype(ml_dtypes.bfloat16).astype(np.float64), axis, -1)
    blocks = v.reshape(v.shape[:-1] + (-1, 32))
    amax = np.abs(blocks).max(-1, keepdims=True)
    byte = np.maximum(np.where(amax > 0, np.frexp(amax)[1] - 1 + 127, 0) - down, 1)
    scale = np.exp2(byte - 127.0)
    codes = (blocks / scale).astype(np.float32).astype(dtype).astype(np.float64)
    return np.moveaxis((codes * scale).reshape(v.shape), -1, axis)


WIDE = False


def mx_kscale(k):
    if not WIDE:
        return np.ones(k)
    levels = np.array([10, -10, 5, -5, 0])
    if k % 512:
        return np.exp2(np.random.permutation(np.resize(levels, k // 32))).repeat(32)
    a = np.empty((k // 512, 16))
    for p in range(k // 512):
        a[p, :8] = np.random.permutation(np.resize(levels, 8))
        for g in range(8):
            far = levels[np.abs(levels - a[p, g]) >= 10]
            a[p, g + 8] = far[np.random.randint(len(far))]
    return np.exp2(a.ravel()).repeat(32)


def f64(x):
    return np.asarray(x).astype(np.float64)


def striped(idx):
    return np.tile(idx.reshape(-1, 16).T, (8, 1)).astype(np.uint16)


def unstriped(offs):
    return offs[:16].T.reshape(-1).astype(np.int64)


def striped8(idx):
    return np.concatenate([x.reshape(-1, 16).T for x in idx]).astype(np.uint16)


def runs(offs, k):
    lists = np.stack([offs[16 * r : 16 * r + 16].T.reshape(-1) for r in range(8)]).astype(np.int64)
    return lists[np.arange(k) % 512 // 64]


def pack_weight(w):
    k, n = w.shape
    w = f64(np.asarray(w, np.float32).astype(ml_dtypes.bfloat16)).reshape(k // 32, 32, n)
    amax = np.abs(w).max(1)
    byte = np.clip(np.where(amax > 0, np.frexp(amax)[1] - 1 + 127 - 7, 1), 1, 254)
    scaled = (w * np.exp2(127.0 - byte)[:, None, :]).reshape(k, n).astype(np.float32)
    words = np.ascontiguousarray(scaled.reshape(k // 512, 128, 4, n).transpose(0, 1, 3, 2)).astype(ml_dtypes.float8_e4m3fn).view(np.uint8)
    return words, np.ascontiguousarray(byte.astype(np.uint8).reshape(k // 512, 16, n))


def unpack_weight(words, scales):
    g, p, n, _ = words.shape
    vals = np.ascontiguousarray(words).view(ml_dtypes.float8_e4m3fn).astype(np.float64) * np.repeat(np.exp2(scales.astype(np.float64) - 127.0), 8, axis=1)[..., None]
    return vals.transpose(0, 1, 3, 2).reshape(g * 512, n)


K, T, S, N, G, H, W = 512, 2048, 512, 512, 2048, 512, 256


def setup_inputs():
    n = np.random.standard_normal
    s = mx_kscale(K)[:, None]
    u = mx_kscale(S)
    packed_xT = pack_weight(n((K, T)) * s)
    packed_dT = pack_weight(n((K, G)) / s)
    perm = np.stack([np.random.permutation(S) for _ in range(8)])
    return {
        "x_words": packed_xT[0],
        "x_scales": packed_xT[1],
        "d_words": packed_dT[0],
        "d_scales": packed_dT[1],
        "gn": (np.random.uniform(0.5, 1.5, (H, 1)) * u[:, None]).astype(np.float32),
        "w1": (n((H, N)) / np.sqrt(H) / u[:, None]).astype(np.float32),
        "offs": striped(np.random.permutation(T)[:S]),
        "kidx": striped8(np.random.randint(0, G, (8, H))),
        "n1": striped8(np.stack([np.random.permutation(S) for _ in range(8)])),
        "n2": striped8(np.stack([np.random.permutation(S) for _ in range(8)])),
        "n3": striped8(perm[:, :W]),
        "n4": striped8(perm[:, W:]),
    }


def reference(x_words, x_scales, d_words, d_scales, gn, w1, offs, kidx, n1, n2, n3, n4):
    d_kidx = unpack_weight(d_words, d_scales)[np.arange(K)[:, None], runs(kidx, K)]
    xq = unpack_weight(x_words, x_scales)[:, unstriped(offs)]
    s = 0.0625 * (d_kidx.T @ xq)
    z = f64(gn) * (0.75 * ((s - (s[np.arange(H)[:, None], runs(n1, H)])) * (s - (s[np.arange(H)[:, None], runs(n2, H)]))))
    h = mxq(f64(w1), 0, "e4m3").T @ mxq(z, 0, "e4m3")
    pa = h[np.arange(N)[:, None], runs(n3, N)]
    pb = h[np.arange(N)[:, None], runs(n4, N)]
    rb = pa * pb
    ra = pa + pb
    ds = np.zeros((N, S))
    ds[np.arange(N)[:, None], runs(n3, N)] = ra
    out = ds.copy()
    out[np.arange(N)[:, None], runs(n4, N)] = rb
    return out

@@ -1,0 +1,176 @@
+from contextlib import ExitStack
+
+import concourse.mybir as mybir
+
+F32 = mybir.dt.float32
+BF16 = mybir.dt.bfloat16
+I32 = mybir.dt.int32
+U32 = mybir.dt.uint32
+U16 = mybir.dt.uint16
+U8 = mybir.dt.uint8
+FP8X4 = mybir.dt.float8_e4m3fn_x4
+ALU = mybir.AluOpType
+COPY = mybir.ActivationFunctionType.Copy
+
+P = 128
+PACK = 4
+TABLE = 2048
+COLS = 512
+HALF = 256
+PAIRS = 256
+FLOPS = 2 * 2 * 512 * 512 * 512
+Z_FACTOR = 0.75 * 0.0625 * 0.0625
+
+
+def tile_picked_keyquadbond_none_p_kernel(
+    tc, x_words, x_scales, d_words, d_scales, gn, w1, offs, kidx, n1, n2, n3, n4, out
+):
+    nc = tc.nc
+    with ExitStack() as ctx:
+        lists = ctx.enter_context(tc.tile_pool(name="lists", bufs=1))
+        keep = ctx.enter_context(tc.tile_pool(name="keep", bufs=1))
+        psum = ctx.enter_context(tc.psum_pool(name="psum", bufs=1))
+
+        def load_list(name, src):
+            held = lists.tile(list(src.shape), U16, name=name)
+            nc.sync.dma_start(held[:], src)
+            return held
+
+        def load_words(name, src):
+            table = keep.tile([P, TABLE], I32, name=name)
+            nc.sync.dma_start(table[:], src[0].rearrange("p c r -> p (c r)").bitcast(I32))
+            return table
+
+        d_byte_table = keep.tile([P, TABLE], U8, name="d_byte_table")
+        x_byte_table = keep.tile([P, TABLE], U8, name="x_byte_table", tag="x_bytes_then_w")
+        nc.vector.memset(d_byte_table[:].bitcast(I32), 0)
+        nc.vector.memset(x_byte_table[:].bitcast(I32), 0)
+
+        kidx_sb = load_list("kidx_sb", kidx)
+        nc.scalar.dma_start(d_byte_table[0:P:8, :].bitcast(I32), d_scales[0].bitcast(I32))
+        d_word_table = load_words("d_word_table", d_words)
+        offs_sb = load_list("offs_sb", offs)
+        for q in range(4):
+            nc.scalar.dma_start(
+                x_byte_table[32 * q : 32 * q + 4, :].bitcast(I32), x_scales[0, 4 * q : 4 * q + 4, :].bitcast(I32)
+            )
+        n1_sb = load_list("n1_sb", n1)
+        n2_sb = load_list("n2_sb", n2)
+        n3_sb = load_list("n3_sb", n3)
+        n4_sb = load_list("n4_sb", n4)
+        x_word_table = load_words("x_word_table", x_words)
+        gain = keep.tile([P, PACK], F32, name="gain")
+        nc.gpsimd.dma_start(gain[:], gn.rearrange("(p t) o -> p (t o)", t=PACK))
+
+        factor = keep.tile([P, PACK], F32, name="factor")
+        nc.scalar.activation(factor[:], gain[:], COPY, scale=Z_FACTOR)
+
+        d_bytes = keep.tile([P, COLS], U8, name="d_bytes", align_bytes=64)
+        nc.vector.tensor_copy(d_bytes[:], d_byte_table[:].indirect(kidx_sb[:]))
+        key_scales = keep.tile([P, COLS], U8, name="key_scales", align_bytes=64)
+        nc.vector.tensor_copy(
+            key_scales[:].rearrange("p (t m) -> p m t", t=PACK), d_bytes[:].rearrange("p (m t) -> p m t", t=PACK)
+        )
+        for c in range(1, 4):
+            nc.scalar.dma_start(key_scales[c:P:32, :].bitcast(I32), key_scales[8 * c : P : 32, :].bitcast(I32))
+
+        d_codes = keep.tile([P, COLS], U32, name="d_codes", align_bytes=64)
+        nc.vector.tensor_copy(d_codes[:], d_word_table[:].bitcast(U32).indirect(kidx_sb[:]))
+        key_codes = keep.tile([P, COLS], U32, name="key_codes", align_bytes=64)
+        nc.vector.tensor_copy(
+            key_codes[:].rearrange("p (t m) -> p m t", t=PACK), d_codes[:].rearrange("p (m t) -> p m t", t=PACK)
+        )
+
+        query_scales = keep.tile([P, COLS], U8, name="query_scales", align_bytes=64)
+        nc.vector.tensor_copy(query_scales[:], x_byte_table[:].indirect(offs_sb[:]))
+
+        w_raw = keep.tile([P, PACK, COLS], F32, name="w_raw", tag="x_bytes_then_w")
+        nc.sync.dma_start(w_raw[:], w1.rearrange("(p j) c -> p j c", j=PACK))
+
+        score_window = [keep.tile([P, COLS], F32, name="score_window%d" % t) for t in range(PACK)]
+        score_plain = [keep.tile([P, COLS], F32, name="score_plain%d" % t) for t in range(PACK)]
+        score_banks = {}
+        for half in range(2):
+            cols = slice(half * HALF, (half + 1) * HALF)
+            query_codes = keep.tile([P, HALF], U32, name="query_codes%d" % half, align_bytes=64)
+            nc.vector.tensor_copy(
+                query_codes[:], x_word_table[:].bitcast(U32).indirect(offs_sb[:, half * 16 : (half + 1) * 16])
+            )
+            for t in range(PACK):
+                rows = slice(t * P, (t + 1) * P)
+                bank = psum.tile([P, HALF], F32, name="bank%d" % (half * PACK + t))
+                nc.tensor.matmul_mx(
+                    out=bank[:],
+                    lhsT=key_codes[:, rows].bitcast(FP8X4),
+                    lhsT_scale=key_scales[:, rows],
+                    rhs=query_codes[:].bitcast(FP8X4),
+                    rhs_scale=query_scales[:, cols],
+                    start=True,
+                    stop=True,
+                )
+                score_banks[half, t] = bank
+        for t in range(PACK):
+            nc.scalar.copy(score_window[t][:, 0:HALF], score_banks[0, t][:])
+            nc.scalar.copy(score_plain[t][:, 0:HALF], score_banks[0, t][:])
+            nc.scalar.copy(score_window[t][:, HALF:COLS], score_banks[1, t][:])
+        for t in range(PACK):
+            nc.scalar.copy(score_plain[t][:, HALF:COLS], score_banks[1, t][:])
+
+        w_grouped = keep.tile([P, PACK * COLS], BF16, name="w_grouped", align_bytes=64)
+        nc.scalar.copy(
+            w_grouped[:].rearrange("p (t m j) -> p m j t", t=PACK, j=PACK),
+            w_raw[:].rearrange("p j (m t) -> p m j t", t=PACK),
+        )
+        w_codes = keep.tile([P, COLS], U32, name="w_codes", align_bytes=64)
+        w_scales = keep.tile([P, COLS], U8, name="w_scales", align_bytes=64)
+        nc.vector.quantize_mx(out=w_codes[:].bitcast(FP8X4), scales=w_scales[:], in_=w_grouped[:])
+
+        h_window = [keep.tile([P, COLS], F32, name="h_window%d" % t) for t in range(PACK)]
+        for half in range(2):
+            cols = slice(half * HALF, (half + 1) * HALF)
+            entries = slice(half * 16, (half + 1) * 16)
+            first = keep.tile([P, PACK, HALF], F32, name="first%d" % half)
+            weighted = keep.tile([P, PACK, HALF], F32, name="weighted%d" % half)
+            second = keep.tile([P, PACK, HALF], F32, name="second%d" % half)
+            for t in range(PACK):
+                nc.vector.tensor_tensor(
+                    first[:, t, :], score_window[t][:].indirect(n1_sb[:, entries]), score_plain[t][:, cols], ALU.subtract
+                )
+                nc.scalar.activation(weighted[:, t, :], first[:, t, :], COPY, scale=factor[:, t : t + 1])
+                nc.vector.tensor_tensor(
+                    second[:, t, :], score_window[t][:].indirect(n2_sb[:, entries]), score_plain[t][:, cols], ALU.subtract
+                )
+            z_grouped = keep.tile([P, HALF * PACK], BF16, name="z_grouped%d" % half, align_bytes=64)
+            nc.vector.tensor_tensor(
+                z_grouped[:].rearrange("p (c i t) -> p c t i", i=4, t=PACK),
+                weighted[:].rearrange("p t (c i) -> p c t i", i=4),
+                second[:].rearrange("p t (c i) -> p c t i", i=4),
+                ALU.mult,
+            )
+            z_codes = keep.tile([P, HALF], U32, name="z_codes%d" % half, align_bytes=64)
+            z_scales = keep.tile([P, HALF], U8, name="z_scales%d" % half, align_bytes=64)
+            nc.vector.quantize_mx(out=z_codes[:].bitcast(FP8X4), scales=z_scales[:], in_=z_grouped[:])
+            for t in range(PACK):
+                rows = slice(t * P, (t + 1) * P)
+                bank = psum.tile([P, HALF], F32, name="bank%d" % (half * PACK + t))
+                nc.tensor.matmul_mx(
+                    out=bank[:],
+                    lhsT=w_codes[:, rows].bitcast(FP8X4),
+                    lhsT_scale=w_scales[:, rows],
+                    rhs=z_codes[:].bitcast(FP8X4),
+                    rhs_scale=z_scales[:],
+                    start=True,
+                    stop=True,
+                )
+                nc.scalar.copy(h_window[t][:, cols], bank[:])
+
+        out_rows = out.rearrange("(p t) c -> p t c", t=PACK)
+        for t in range(PACK):
+            pa = keep.tile([P, PAIRS], F32, name="pa%d" % t)
+            pb = keep.tile([P, PAIRS], F32, name="pb%d" % t)
+            nc.vector.tensor_copy(pa[:], h_window[t][:].indirect(n3_sb[:]))
+            nc.vector.tensor_copy(pb[:], h_window[t][:].indirect(n4_sb[:]))
+            bonded = keep.tile([P, COLS], F32, name="bonded%d" % t)
+            nc.vector.tensor_tensor(bonded[:].indirect(n3_sb[:]), pa[:], pb[:], ALU.add)
+            nc.vector.tensor_tensor(bonded[:].indirect(n4_sb[:]), pa[:], pb[:], ALU.mult)
+            nc.sync.dma_start(out_rows[:, t, :], bonded[:])

@@ -47,32 +47,31 @@ def tile_picked_keyquadbond_none_p_kernel(
         nc.vector.memset(x_byte_table[:].bitcast(I32), 0)
 
         kidx_sb = load_list("kidx_sb", kidx)
-        nc.scalar.dma_start(d_byte_table[0:P:8, :].bitcast(I32), d_scales[0].bitcast(I32))
-        d_word_table = load_words("d_word_table", d_words)
+        nc.sync.dma_start(d_byte_table[0:P:8, :].bitcast(I32), d_scales[0].bitcast(I32))
         offs_sb = load_list("offs_sb", offs)
+        d_word_table = load_words("d_word_table", d_words)
         for q in range(4):
-            nc.scalar.dma_start(
+            nc.sync.dma_start(
                 x_byte_table[32 * q : 32 * q + 4, :].bitcast(I32), x_scales[0, 4 * q : 4 * q + 4, :].bitcast(I32)
             )
+        x_word_table = load_words("x_word_table", x_words)
+
+        d_bytes = keep.tile([P, COLS], U8, name="d_bytes", align_bytes=64, tag="d_bytes_then_gain")
+        nc.vector.tensor_copy(d_bytes[:], d_byte_table[:].indirect(kidx_sb[:]))
+        key_scales = keep.tile([P, COLS], U8, name="key_scales", align_bytes=64)
+        nc.vector.tensor_copy(
+            key_scales[:].rearrange("p (t m) -> p t m", t=PACK), d_bytes[:].rearrange("p (m t) -> p t m", t=PACK)
+        )
+        for c in range(1, 4):
+            nc.sync.dma_start(key_scales[c:P:32, :].bitcast(I32), key_scales[8 * c : P : 32, :].bitcast(I32))
         n1_sb = load_list("n1_sb", n1)
         n2_sb = load_list("n2_sb", n2)
         n3_sb = load_list("n3_sb", n3)
         n4_sb = load_list("n4_sb", n4)
-        x_word_table = load_words("x_word_table", x_words)
-        gain = keep.tile([P, PACK], F32, name="gain")
-        nc.gpsimd.dma_start(gain[:], gn.rearrange("(p t) o -> p (t o)", t=PACK))
-
+        gain = keep.tile([P, PACK], F32, name="gain", align_bytes=64, tag="d_bytes_then_gain")
+        nc.sync.dma_start(gain[:], gn.rearrange("(p t) o -> p (t o)", t=PACK))
         factor = keep.tile([P, PACK], F32, name="factor")
-        nc.scalar.activation(factor[:], gain[:], COPY, scale=Z_FACTOR)
-
-        d_bytes = keep.tile([P, COLS], U8, name="d_bytes", align_bytes=64)
-        nc.vector.tensor_copy(d_bytes[:], d_byte_table[:].indirect(kidx_sb[:]))
-        key_scales = keep.tile([P, COLS], U8, name="key_scales", align_bytes=64)
-        nc.vector.tensor_copy(
-            key_scales[:].rearrange("p (t m) -> p m t", t=PACK), d_bytes[:].rearrange("p (m t) -> p m t", t=PACK)
-        )
-        for c in range(1, 4):
-            nc.scalar.dma_start(key_scales[c:P:32, :].bitcast(I32), key_scales[8 * c : P : 32, :].bitcast(I32))
+        nc.gpsimd.tensor_scalar(factor[:], gain[:], Z_FACTOR, 0.0, ALU.mult, ALU.add)
 
         d_codes = keep.tile([P, COLS], U32, name="d_codes", align_bytes=64)
         nc.vector.tensor_copy(d_codes[:], d_word_table[:].bitcast(U32).indirect(kidx_sb[:]))
@@ -89,70 +88,59 @@ def tile_picked_keyquadbond_none_p_kernel(
 
         score_window = [keep.tile([P, COLS], F32, name="score_window%d" % t) for t in range(PACK)]
         score_plain = [keep.tile([P, COLS], F32, name="score_plain%d" % t) for t in range(PACK)]
-        score_banks = {}
+        query_codes = [keep.tile([P, HALF], U32, name="query_codes%d" % half, align_bytes=64) for half in range(2)]
         for half in range(2):
-            cols = slice(half * HALF, (half + 1) * HALF)
-            query_codes = keep.tile([P, HALF], U32, name="query_codes%d" % half, align_bytes=64)
             nc.vector.tensor_copy(
-                query_codes[:], x_word_table[:].bitcast(U32).indirect(offs_sb[:, half * 16 : (half + 1) * 16])
+                query_codes[half][:], x_word_table[:].bitcast(U32).indirect(offs_sb[:, half * 16 : (half + 1) * 16])
             )
-            for t in range(PACK):
-                rows = slice(t * P, (t + 1) * P)
-                bank = psum.tile([P, HALF], F32, name="bank%d" % (half * PACK + t))
+        halves = [(slice(h * HALF, (h + 1) * HALF), slice(h * 16, (h + 1) * 16)) for h in range(2)]
+        score_banks = {}
+        for t in range(PACK):
+            rows = slice(t * P, (t + 1) * P)
+            for half, (cols, entries) in enumerate(halves):
+                bank = psum.tile([P, HALF], F32, name="bank%d" % (2 * t + half))
                 nc.tensor.matmul_mx(
                     out=bank[:],
                     lhsT=key_codes[:, rows].bitcast(FP8X4),
                     lhsT_scale=key_scales[:, rows],
-                    rhs=query_codes[:].bitcast(FP8X4),
+                    rhs=query_codes[half][:].bitcast(FP8X4),
                     rhs_scale=query_scales[:, cols],
                     start=True,
                     stop=True,
                 )
-                score_banks[half, t] = bank
-        for t in range(PACK):
-            nc.scalar.copy(score_window[t][:, 0:HALF], score_banks[0, t][:])
-            nc.scalar.copy(score_plain[t][:, 0:HALF], score_banks[0, t][:])
-            nc.scalar.copy(score_window[t][:, HALF:COLS], score_banks[1, t][:])
-        for t in range(PACK):
-            nc.scalar.copy(score_plain[t][:, HALF:COLS], score_banks[1, t][:])
+                score_banks[t, half] = bank
+            nc.scalar.copy(score_window[t][:, 0:HALF], score_banks[t, 0][:])
+            nc.scalar.copy(score_plain[t][:, 0:HALF], score_banks[t, 0][:])
+            nc.scalar.copy(score_window[t][:, HALF:COLS], score_banks[t, 1][:])
 
-        w_grouped = keep.tile([P, PACK * COLS], BF16, name="w_grouped", align_bytes=64)
-        nc.scalar.copy(
-            w_grouped[:].rearrange("p (t m j) -> p m j t", t=PACK, j=PACK),
-            w_raw[:].rearrange("p j (m t) -> p m j t", t=PACK),
-        )
-        w_codes = keep.tile([P, COLS], U32, name="w_codes", align_bytes=64)
-        w_scales = keep.tile([P, COLS], U8, name="w_scales", align_bytes=64)
-        nc.vector.quantize_mx(out=w_codes[:].bitcast(FP8X4), scales=w_scales[:], in_=w_grouped[:])
+        def difference(dst, t, offsets, half):
+            cols, entries = halves[half]
+            nc.vector.tensor_tensor(
+                dst[:, t, :], score_window[t][:].indirect(offsets[:, entries]), score_plain[t][:, cols], ALU.subtract
+            )
 
-        h_window = [keep.tile([P, COLS], F32, name="h_window%d" % t) for t in range(PACK)]
-        for half in range(2):
-            cols = slice(half * HALF, (half + 1) * HALF)
-            entries = slice(half * 16, (half + 1) * 16)
-            first = keep.tile([P, PACK, HALF], F32, name="first%d" % half)
-            weighted = keep.tile([P, PACK, HALF], F32, name="weighted%d" % half)
-            second = keep.tile([P, PACK, HALF], F32, name="second%d" % half)
-            for t in range(PACK):
-                nc.vector.tensor_tensor(
-                    first[:, t, :], score_window[t][:].indirect(n1_sb[:, entries]), score_plain[t][:, cols], ALU.subtract
-                )
-                nc.scalar.activation(weighted[:, t, :], first[:, t, :], COPY, scale=factor[:, t : t + 1])
-                nc.vector.tensor_tensor(
-                    second[:, t, :], score_window[t][:].indirect(n2_sb[:, entries]), score_plain[t][:, cols], ALU.subtract
-                )
+        def weigh(dst, src, t):
+            nc.scalar.activation(dst[:, t, :], src[:, t, :], COPY, scale=factor[:, t : t + 1])
+
+        def quantise_z(weighted, second, half):
             z_grouped = keep.tile([P, HALF * PACK], BF16, name="z_grouped%d" % half, align_bytes=64)
             nc.vector.tensor_tensor(
-                z_grouped[:].rearrange("p (c i t) -> p c t i", i=4, t=PACK),
-                weighted[:].rearrange("p t (c i) -> p c t i", i=4),
-                second[:].rearrange("p t (c i) -> p c t i", i=4),
+                z_grouped[:].rearrange("p (c i t) -> p c t i", i=2, t=PACK),
+                weighted[:].rearrange("p t (c i) -> p c t i", i=2),
+                second[:].rearrange("p t (c i) -> p c t i", i=2),
                 ALU.mult,
             )
             z_codes = keep.tile([P, HALF], U32, name="z_codes%d" % half, align_bytes=64)
             z_scales = keep.tile([P, HALF], U8, name="z_scales%d" % half, align_bytes=64)
             nc.vector.quantize_mx(out=z_codes[:].bitcast(FP8X4), scales=z_scales[:], in_=z_grouped[:])
+            return z_codes, z_scales
+
+        h_window = [keep.tile([P, COLS], F32, name="h_window%d" % t) for t in range(PACK)]
+
+        def second_product(z_codes, z_scales, half):
             for t in range(PACK):
                 rows = slice(t * P, (t + 1) * P)
-                bank = psum.tile([P, HALF], F32, name="bank%d" % (half * PACK + t))
+                bank = psum.tile([P, HALF], F32, name="bank%d" % (2 * t + half))
                 nc.tensor.matmul_mx(
                     out=bank[:],
                     lhsT=w_codes[:, rows].bitcast(FP8X4),
@@ -162,15 +150,47 @@ def tile_picked_keyquadbond_none_p_kernel(
                     start=True,
                     stop=True,
                 )
-                nc.scalar.copy(h_window[t][:, cols], bank[:])
+                nc.scalar.copy(h_window[t][:, halves[half][0]], bank[:])
 
-        out_rows = out.rearrange("(p t) c -> p t c", t=PACK)
+        first = [keep.tile([P, PACK, HALF], F32, name="first%d" % half) for half in range(2)]
+        weighted = [keep.tile([P, PACK, HALF], F32, name="weighted0")]
+        second = keep.tile([P, PACK, HALF], F32, name="second0")
         for t in range(PACK):
-            pa = keep.tile([P, PAIRS], F32, name="pa%d" % t)
-            pb = keep.tile([P, PAIRS], F32, name="pb%d" % t)
-            nc.vector.tensor_copy(pa[:], h_window[t][:].indirect(n3_sb[:]))
-            nc.vector.tensor_copy(pb[:], h_window[t][:].indirect(n4_sb[:]))
-            bonded = keep.tile([P, COLS], F32, name="bonded%d" % t)
-            nc.vector.tensor_tensor(bonded[:].indirect(n3_sb[:]), pa[:], pb[:], ALU.add)
-            nc.vector.tensor_tensor(bonded[:].indirect(n4_sb[:]), pa[:], pb[:], ALU.mult)
-            nc.sync.dma_start(out_rows[:, t, :], bonded[:])
+            difference(first[0], t, n1_sb, 0)
+            weigh(weighted[0], first[0], t)
+            difference(second, t, n2_sb, 0)
+        z_low = quantise_z(weighted[0], second, 0)
+
+        w_grouped = keep.tile([P, PACK * COLS], BF16, name="w_grouped", align_bytes=64, tag="w_then_second")
+        nc.scalar.copy(
+            w_grouped[:].rearrange("p (t m j) -> p m j t", t=PACK, j=PACK),
+            w_raw[:].rearrange("p j (m t) -> p m j t", t=PACK),
+        )
+        w_codes = keep.tile([P, COLS], U32, name="w_codes", align_bytes=64)
+        w_scales = keep.tile([P, COLS], U8, name="w_scales", align_bytes=64)
+        nc.vector.quantize_mx(out=w_codes[:].bitcast(FP8X4), scales=w_scales[:], in_=w_grouped[:])
+
+        weighted.append(keep.tile([P, PACK, HALF], F32, name="weighted1", tag="x_bytes_then_w"))
+        for t in range(PACK):
+            nc.scalar.copy(score_plain[t][:, HALF:COLS], score_banks[t, 1][:])
+            difference(first[1], t, n1_sb, 1)
+            weigh(weighted[1], first[1], t)
+        second_product(*z_low, 0)
+        second = keep.tile([P, PACK, HALF], F32, name="second1", align_bytes=64, tag="w_then_second")
+        for t in range(PACK):
+            difference(second, t, n2_sb, 1)
+        second_product(*quantise_z(weighted[1], second, 1), 1)
+
+        pa = [keep.tile([P, PAIRS], F32, name="pa%d" % t) for t in range(PACK)]
+        pb = [keep.tile([P, PAIRS], F32, name="pb%d" % t) for t in range(PACK)]
+        for t in range(PACK):
+            nc.vector.tensor_copy(pa[t][:], h_window[t][:].indirect(n3_sb[:]))
+            nc.vector.tensor_copy(pb[t][:], h_window[t][:].indirect(n4_sb[:]))
+        out_rows = out.rearrange("(p t) c -> p t c", t=PACK)
+        bonded = [keep.tile([P, COLS], F32, name="bonded%d" % t) for t in range(PACK)]
+        for pair in ((0, 1), (2, 3)):
+            for t in pair:
+                nc.vector.tensor_tensor(bonded[t][:].indirect(n3_sb[:]), pa[t][:], pb[t][:], ALU.add)
+            for t in pair:
+                nc.vector.tensor_tensor(bonded[t][:].indirect(n4_sb[:]), pa[t][:], pb[t][:], ALU.mult)
+                nc.sync.dma_start(out_rows[:, t, :], bonded[t][:])

@@ -86,8 +86,10 @@ def tile_picked_keyquadbond_none_p_kernel(
         w_raw = keep.tile([P, PACK, COLS], F32, name="w_raw", tag="x_bytes_then_w")
         nc.sync.dma_start(w_raw[:], w1.rearrange("(p j) c -> p j c", j=PACK))
 
-        score_window = [keep.tile([P, COLS], F32, name="score_window%d" % t) for t in range(PACK)]
-        score_plain = [keep.tile([P, COLS], F32, name="score_plain%d" % t) for t in range(PACK)]
+        score_window = [keep.tile([P, 2 * COLS], F32, name="score_window%d" % t) for t in range(PACK)]
+        nc.vector.memset(score_window[0][:, COLS:], 0.0)
+        last_plain = keep.tile([P, COLS], F32, name="last_plain")
+        score_plain = [score_window[t + 1][:, COLS:] for t in range(PACK - 1)] + [last_plain[:]]
         query_codes = [keep.tile([P, HALF], U32, name="query_codes%d" % half, align_bytes=64) for half in range(2)]
         for half in range(2):
             nc.vector.tensor_copy(
@@ -112,74 +114,63 @@ def tile_picked_keyquadbond_none_p_kernel(
             nc.scalar.copy(score_window[t][:, 0:HALF], score_banks[t, 0][:])
             nc.scalar.copy(score_plain[t][:, 0:HALF], score_banks[t, 0][:])
             nc.scalar.copy(score_window[t][:, HALF:COLS], score_banks[t, 1][:])
+            nc.scalar.copy(score_plain[t][:, HALF:COLS], score_banks[t, 1][:])
 
-        def difference(dst, t, offsets, half):
-            cols, entries = halves[half]
-            nc.vector.tensor_tensor(
-                dst[:, t, :], score_window[t][:].indirect(offsets[:, entries]), score_plain[t][:, cols], ALU.subtract
-            )
+        def difference(dst, t, offsets, cols):
+            nc.vector.tensor_tensor(dst, score_window[t][:].indirect(offsets), score_plain[t][:, cols], ALU.subtract)
 
-        def weigh(dst, src, t):
-            nc.scalar.activation(dst[:, t, :], src[:, t, :], COPY, scale=factor[:, t : t + 1])
+        first = keep.tile([P, PACK, COLS], F32, name="first")
+        weighted = keep.tile([P, PACK, COLS], F32, name="weighted")
+        second = keep.tile([P, PACK, COLS], F32, name="second")
+        whole = [(slice(0, COLS), slice(0, COLS // 16))]
 
-        def quantise_z(weighted, second, half):
-            z_grouped = keep.tile([P, HALF * PACK], BF16, name="z_grouped%d" % half, align_bytes=64)
-            nc.vector.tensor_tensor(
-                z_grouped[:].rearrange("p (c i t) -> p c t i", i=2, t=PACK),
-                weighted[:].rearrange("p t (c i) -> p c t i", i=2),
-                second[:].rearrange("p t (c i) -> p c t i", i=2),
-                ALU.mult,
-            )
-            z_codes = keep.tile([P, HALF], U32, name="z_codes%d" % half, align_bytes=64)
-            z_scales = keep.tile([P, HALF], U8, name="z_scales%d" % half, align_bytes=64)
-            nc.vector.quantize_mx(out=z_codes[:].bitcast(FP8X4), scales=z_scales[:], in_=z_grouped[:])
-            return z_codes, z_scales
+        def key_tile(t):
+            difference(first[:, t, :], t, n1_sb[:], slice(0, COLS))
+            nc.scalar.activation(weighted[:, t, :], first[:, t, :], COPY, scale=factor[:, t : t + 1])
+            for cols, entries in halves if t == 0 else whole:
+                difference(second[:, t, cols], t, n2_sb[:, entries], cols)
 
-        h_window = [keep.tile([P, COLS], F32, name="h_window%d" % t) for t in range(PACK)]
-
-        def second_product(z_codes, z_scales, half):
-            for t in range(PACK):
-                rows = slice(t * P, (t + 1) * P)
-                bank = psum.tile([P, HALF], F32, name="bank%d" % (2 * t + half))
-                nc.tensor.matmul_mx(
-                    out=bank[:],
-                    lhsT=w_codes[:, rows].bitcast(FP8X4),
-                    lhsT_scale=w_scales[:, rows],
-                    rhs=z_codes[:].bitcast(FP8X4),
-                    rhs_scale=z_scales[:],
-                    start=True,
-                    stop=True,
-                )
-                nc.scalar.copy(h_window[t][:, halves[half][0]], bank[:])
-
-        first = [keep.tile([P, PACK, HALF], F32, name="first%d" % half) for half in range(2)]
-        weighted = [keep.tile([P, PACK, HALF], F32, name="weighted0")]
-        second = keep.tile([P, PACK, HALF], F32, name="second0")
-        for t in range(PACK):
-            difference(first[0], t, n1_sb, 0)
-            weigh(weighted[0], first[0], t)
-            difference(second, t, n2_sb, 0)
-        z_low = quantise_z(weighted[0], second, 0)
-
-        w_grouped = keep.tile([P, PACK * COLS], BF16, name="w_grouped", align_bytes=64, tag="w_then_second")
+        key_tile(0)
+        key_tile(1)
+        w_grouped = keep.tile([P, PACK * COLS], BF16, name="w_grouped", align_bytes=64)
         nc.scalar.copy(
             w_grouped[:].rearrange("p (t m j) -> p m j t", t=PACK, j=PACK),
             w_raw[:].rearrange("p j (m t) -> p m j t", t=PACK),
         )
+        key_tile(2)
+        key_tile(3)
         w_codes = keep.tile([P, COLS], U32, name="w_codes", align_bytes=64)
         w_scales = keep.tile([P, COLS], U8, name="w_scales", align_bytes=64)
         nc.vector.quantize_mx(out=w_codes[:].bitcast(FP8X4), scales=w_scales[:], in_=w_grouped[:])
 
-        weighted.append(keep.tile([P, PACK, HALF], F32, name="weighted1", tag="x_bytes_then_w"))
+        z_grouped = [keep.tile([P, HALF * PACK], BF16, name="z_grouped%d" % half, align_bytes=64) for half in range(2)]
+        z_codes = [keep.tile([P, HALF], U32, name="z_codes%d" % half, align_bytes=64) for half in range(2)]
+        z_scales = [keep.tile([P, HALF], U8, name="z_scales%d" % half, align_bytes=64) for half in range(2)]
+        for half, (cols, entries) in enumerate(halves):
+            nc.vector.tensor_tensor(
+                z_grouped[half][:].rearrange("p (c i t) -> p c t i", i=2, t=PACK),
+                weighted[:, :, cols].rearrange("p t (c i) -> p c t i", i=2),
+                second[:, :, cols].rearrange("p t (c i) -> p c t i", i=2),
+                ALU.mult,
+            )
+        for half in range(2):
+            nc.vector.quantize_mx(out=z_codes[half][:].bitcast(FP8X4), scales=z_scales[half][:], in_=z_grouped[half][:])
+
+        h_window = [keep.tile([P, COLS], F32, name="h_window%d" % t) for t in range(PACK)]
         for t in range(PACK):
-            nc.scalar.copy(score_plain[t][:, HALF:COLS], score_banks[t, 1][:])
-            difference(first[1], t, n1_sb, 1)
-            weigh(weighted[1], first[1], t)
-        second_product(*z_low, 0)
-        second = keep.tile([P, PACK, HALF], F32, name="second1", align_bytes=64, tag="w_then_second")
-        for t in range(PACK):
-            difference(second, t, n2_sb, 1)
-        second_product(*quantise_z(weighted[1], second, 1), 1)
+            rows = slice(t * P, (t + 1) * P)
+            for half, (cols, entries) in enumerate(halves):
+                bank = psum.tile([P, HALF], F32, name="bank%d" % (2 * t + 1 if half else t % 2))
+                nc.tensor.matmul_mx(
+                    out=bank[:],
+                    lhsT=w_codes[:, rows].bitcast(FP8X4),
+                    lhsT_scale=w_scales[:, rows],
+                    rhs=z_codes[half][:].bitcast(FP8X4),
+                    rhs_scale=z_scales[half][:],
+                    start=True,
+                    stop=True,
+                )
+                nc.scalar.copy(h_window[t][:, cols], bank[:])
 
         pa = [keep.tile([P, PAIRS], F32, name="pa%d" % t) for t in range(PACK)]
         pb = [keep.tile([P, PAIRS], F32, name="pb%d" % t) for t in range(PACK)]

from contextlib import ExitStack

import concourse.mybir as mybir

F32 = mybir.dt.float32
BF16 = mybir.dt.bfloat16
I32 = mybir.dt.int32
U32 = mybir.dt.uint32
U16 = mybir.dt.uint16
U8 = mybir.dt.uint8
FP8X4 = mybir.dt.float8_e4m3fn_x4
ALU = mybir.AluOpType
COPY = mybir.ActivationFunctionType.Copy

P = 128
PACK = 4
TABLE = 2048
COLS = 512
HALF = 256
PAIRS = 256
FLOPS = 2 * 2 * 512 * 512 * 512
Z_FACTOR = 0.75 * 0.0625 * 0.0625


def tile_picked_keyquadbond_none_p_kernel(
    tc, x_words, x_scales, d_words, d_scales, gn, w1, offs, kidx, n1, n2, n3, n4, out
):
    nc = tc.nc
    with ExitStack() as ctx:
        lists = ctx.enter_context(tc.tile_pool(name="lists", bufs=1))
        keep = ctx.enter_context(tc.tile_pool(name="keep", bufs=1))
        psum = ctx.enter_context(tc.psum_pool(name="psum", bufs=1))

        def load_list(name, src):
            held = lists.tile(list(src.shape), U16, name=name)
            nc.sync.dma_start(held[:], src)
            return held

        def load_words(name, src):
            table = keep.tile([P, TABLE], I32, name=name)
            nc.sync.dma_start(table[:], src[0].rearrange("p c r -> p (c r)").bitcast(I32))
            return table

        d_byte_table = keep.tile([P, TABLE], U8, name="d_byte_table")
        x_byte_table = keep.tile([P, TABLE], U8, name="x_byte_table", tag="x_bytes_then_w")
        nc.vector.memset(d_byte_table[:].bitcast(I32), 0)
        nc.vector.memset(x_byte_table[:].bitcast(I32), 0)

        kidx_sb = load_list("kidx_sb", kidx)
        nc.sync.dma_start(d_byte_table[0:P:8, :].bitcast(I32), d_scales[0].bitcast(I32))
        offs_sb = load_list("offs_sb", offs)
        d_word_table = load_words("d_word_table", d_words)
        for q in range(4):
            nc.sync.dma_start(
                x_byte_table[32 * q : 32 * q + 4, :].bitcast(I32), x_scales[0, 4 * q : 4 * q + 4, :].bitcast(I32)
            )
        x_word_table = load_words("x_word_table", x_words)

        d_bytes = keep.tile([P, COLS], U8, name="d_bytes", align_bytes=64, tag="d_bytes_then_gain")
        nc.vector.tensor_copy(d_bytes[:], d_byte_table[:].indirect(kidx_sb[:]))
        key_scales = keep.tile([P, COLS], U8, name="key_scales", align_bytes=64)
        nc.vector.tensor_copy(
            key_scales[:].rearrange("p (t m) -> p t m", t=PACK), d_bytes[:].rearrange("p (m t) -> p t m", t=PACK)
        )
        for c in range(1, 4):
            nc.sync.dma_start(key_scales[c:P:32, :].bitcast(I32), key_scales[8 * c : P : 32, :].bitcast(I32))
        n1_sb = load_list("n1_sb", n1)
        n2_sb = load_list("n2_sb", n2)
        n3_sb = load_list("n3_sb", n3)
        n4_sb = load_list("n4_sb", n4)
        gain = keep.tile([P, PACK], F32, name="gain", align_bytes=64, tag="d_bytes_then_gain")
        nc.sync.dma_start(gain[:], gn.rearrange("(p t) o -> p (t o)", t=PACK))
        factor = keep.tile([P, PACK], F32, name="factor")
        nc.gpsimd.tensor_scalar(factor[:], gain[:], Z_FACTOR, 0.0, ALU.mult, ALU.add)

        d_codes = keep.tile([P, COLS], U32, name="d_codes", align_bytes=64)
        nc.vector.tensor_copy(d_codes[:], d_word_table[:].bitcast(U32).indirect(kidx_sb[:]))
        key_codes = keep.tile([P, COLS], U32, name="key_codes", align_bytes=64)
        nc.vector.tensor_copy(
            key_codes[:].rearrange("p (t m) -> p m t", t=PACK), d_codes[:].rearrange("p (m t) -> p m t", t=PACK)
        )

        query_scales = keep.tile([P, COLS], U8, name="query_scales", align_bytes=64)
        nc.vector.tensor_copy(query_scales[:], x_byte_table[:].indirect(offs_sb[:]))

        w_raw = keep.tile([P, PACK, COLS], F32, name="w_raw", tag="x_bytes_then_w")
        nc.sync.dma_start(w_raw[:], w1.rearrange("(p j) c -> p j c", j=PACK))

        score_window = [keep.tile([P, 2 * COLS], F32, name="score_window%d" % t) for t in range(PACK)]
        nc.vector.memset(score_window[0][:, COLS:], 0.0)
        last_plain = keep.tile([P, COLS], F32, name="last_plain")
        score_plain = [score_window[t + 1][:, COLS:] for t in range(PACK - 1)] + [last_plain[:]]
        query_codes = [keep.tile([P, HALF], U32, name="query_codes%d" % half, align_bytes=64) for half in range(2)]
        for half in range(2):
            nc.vector.tensor_copy(
                query_codes[half][:], x_word_table[:].bitcast(U32).indirect(offs_sb[:, half * 16 : (half + 1) * 16])
            )
        halves = [(slice(h * HALF, (h + 1) * HALF), slice(h * 16, (h + 1) * 16)) for h in range(2)]
        score_banks = {}
        for t in range(PACK):
            rows = slice(t * P, (t + 1) * P)
            for half, (cols, entries) in enumerate(halves):
                bank = psum.tile([P, HALF], F32, name="bank%d" % (2 * t + half))
                nc.tensor.matmul_mx(
                    out=bank[:],
                    lhsT=key_codes[:, rows].bitcast(FP8X4),
                    lhsT_scale=key_scales[:, rows],
                    rhs=query_codes[half][:].bitcast(FP8X4),
                    rhs_scale=query_scales[:, cols],
                    start=True,
                    stop=True,
                )
                score_banks[t, half] = bank
            nc.scalar.copy(score_window[t][:, 0:HALF], score_banks[t, 0][:])
            nc.scalar.copy(score_plain[t][:, 0:HALF], score_banks[t, 0][:])
            nc.scalar.copy(score_window[t][:, HALF:COLS], score_banks[t, 1][:])
            nc.scalar.copy(score_plain[t][:, HALF:COLS], score_banks[t, 1][:])

        def difference(dst, t, offsets, cols):
            nc.vector.tensor_tensor(dst, score_window[t][:].indirect(offsets), score_plain[t][:, cols], ALU.subtract)

        first = keep.tile([P, PACK, COLS], F32, name="first")
        weighted = keep.tile([P, PACK, COLS], F32, name="weighted")
        second = keep.tile([P, PACK, COLS], F32, name="second")
        whole = [(slice(0, COLS), slice(0, COLS // 16))]

        def key_tile(t):
            difference(first[:, t, :], t, n1_sb[:], slice(0, COLS))
            nc.scalar.activation(weighted[:, t, :], first[:, t, :], COPY, scale=factor[:, t : t + 1])
            for cols, entries in halves if t == 0 else whole:
                difference(second[:, t, cols], t, n2_sb[:, entries], cols)

        key_tile(0)
        key_tile(1)
        w_grouped = keep.tile([P, PACK * COLS], BF16, name="w_grouped", align_bytes=64)
        nc.scalar.copy(
            w_grouped[:].rearrange("p (t m j) -> p m j t", t=PACK, j=PACK),
            w_raw[:].rearrange("p j (m t) -> p m j t", t=PACK),
        )
        key_tile(2)
        key_tile(3)
        w_codes = keep.tile([P, COLS], U32, name="w_codes", align_bytes=64)
        w_scales = keep.tile([P, COLS], U8, name="w_scales", align_bytes=64)
        nc.vector.quantize_mx(out=w_codes[:].bitcast(FP8X4), scales=w_scales[:], in_=w_grouped[:])

        z_grouped = [keep.tile([P, HALF * PACK], BF16, name="z_grouped%d" % half, align_bytes=64) for half in range(2)]
        z_codes = [keep.tile([P, HALF], U32, name="z_codes%d" % half, align_bytes=64) for half in range(2)]
        z_scales = [keep.tile([P, HALF], U8, name="z_scales%d" % half, align_bytes=64) for half in range(2)]
        for half, (cols, entries) in enumerate(halves):
            nc.vector.tensor_tensor(
                z_grouped[half][:].rearrange("p (c i t) -> p c t i", i=2, t=PACK),
                weighted[:, :, cols].rearrange("p t (c i) -> p c t i", i=2),
                second[:, :, cols].rearrange("p t (c i) -> p c t i", i=2),
                ALU.mult,
            )
        for half in range(2):
            nc.vector.quantize_mx(out=z_codes[half][:].bitcast(FP8X4), scales=z_scales[half][:], in_=z_grouped[half][:])

        h_window = [keep.tile([P, COLS], F32, name="h_window%d" % t) for t in range(PACK)]
        for t in range(PACK):
            rows = slice(t * P, (t + 1) * P)
            for half, (cols, entries) in enumerate(halves):
                bank = psum.tile([P, HALF], F32, name="bank%d" % (2 * t + 1 if half else t % 2))
                nc.tensor.matmul_mx(
                    out=bank[:],
                    lhsT=w_codes[:, rows].bitcast(FP8X4),
                    lhsT_scale=w_scales[:, rows],
                    rhs=z_codes[half][:].bitcast(FP8X4),
                    rhs_scale=z_scales[half][:],
                    start=True,
                    stop=True,
                )
                nc.scalar.copy(h_window[t][:, cols], bank[:])

        pa = [keep.tile([P, PAIRS], F32, name="pa%d" % t) for t in range(PACK)]
        pb = [keep.tile([P, PAIRS], F32, name="pb%d" % t) for t in range(PACK)]
        for t in range(PACK):
            nc.vector.tensor_copy(pa[t][:], h_window[t][:].indirect(n3_sb[:]))
            nc.vector.tensor_copy(pb[t][:], h_window[t][:].indirect(n4_sb[:]))
        out_rows = out.rearrange("(p t) c -> p t c", t=PACK)
        bonded = [keep.tile([P, COLS], F32, name="bonded%d" % t) for t in range(PACK)]
        for pair in ((0, 1), (2, 3)):
            for t in pair:
                nc.vector.tensor_tensor(bonded[t][:].indirect(n3_sb[:]), pa[t][:], pb[t][:], ALU.add)
            for t in pair:
                nc.vector.tensor_tensor(bonded[t][:].indirect(n4_sb[:]), pa[t][:], pb[t][:], ALU.mult)
                nc.sync.dma_start(out_rows[:, t, :], bonded[t][:])
